import numpy as np, ml_dtypes
CORES = [3,11,19,27,35,43,51,59]
N = 8
BF = ml_dtypes.bfloat16
S, M = 2048, 512
def pack(x, slot, w):
    return {"x": np.clip(np.rint(x), -255, 255).astype(np.int32).astype(np.float32).astype(BF), "slot": slot.astype(np.int32), "w": np.rint(w).astype(np.int32).astype(np.float32)}
def setup_inputs(rng):
    x = rng.standard_normal((N, 128, S), dtype=np.float32) * rng.integers(20, 61, (1, 128, 1)) + rng.integers(-80, 81, (1, 128, 1)) + rng.integers(-15, 16, (N, 128, 1))
    slot = np.floor(M * rng.random((N, 8, S)) ** rng.integers(1, 4, (1, 8, 1))).astype(np.int64) ^ rng.integers(0, M, (1, 8, 1))
    return pack(x, slot, rng.integers(-255, 256, (N, 128, 1)))
def setup_inputs_one(rng):
    d = setup_inputs(rng); e = rng.integers(0, M, (1, 8, 1)); e[0, 0] = 0; e[0, 7] = M - 1
    d["slot"][:] = e; d["w"].reshape(N, 8, 16)[:, ::2] = 0; return d
def setup_inputs_gaps(rng):
    x = np.floor(255 * rng.random((N, 128, S)) ** 4) - 255
    slot = 2 * rng.integers(0, M // 2, (N, 8, S)) + ((np.arange(N)[:, None, None] + np.arange(8)[:, None]) & 1)
    z = rng.integers(0, M, (1, 8, 1)); slot = np.where(slot == z, slot ^ 2, slot)
    slot[0, :, S - 1] = z[0, :, 0]; slot[N - 1, :, 0] = z[0, :, 0]
    x[0, :, S - 1] = rng.integers(-60, 0, 128); x[N - 1, :, 0] = -255
    return pack(x, slot, rng.integers(-255, 256, (N, 128, 1)))
def setup_inputs_ends(rng):
    p = rng.choice(np.array([0, 2.0 ** -6, 2.0 ** -11]), 128); p[0] = 0; p[1] = 2.0 ** -6
    x = np.where(rng.random((N, 128, S)) < p[:, None], 255, -255)
    slot = rng.integers(0, M, (N, 8, S)); slot[:, 1::2] = rng.choice(np.array([0, 1, M - 2, M - 1]), (N, 4, S))
    w = rng.choice(np.array([-255, 255]), (N, 128, 1)); w[:, :16] = 255
    return pack(x, slot, w)
def setup_inputs_spread(rng):
    x = rng.integers(-255, 256, (N, 128, S)) * np.exp2(-rng.integers(0, 9, (N, 1, S)))
    slot = np.floor(M * rng.random((N, 8, S)) ** rng.integers(1, 13, (N, 8, 1))).astype(np.int64) ^ rng.integers(0, M, (1, 8, 1))
    return pack(x, slot, rng.integers(-255, 256, (N, 128, 1)) * np.exp2(-rng.integers(0, 8, (N, 128, 1))))
def check_inputs(d):
    bad = []
    for k in ("x", "w"):
        v = d[k].astype(np.float32)
        if not (np.all(np.abs(v) <= 255) and np.all(v == np.rint(v))): bad.append(k + " whole, -255 to 255")
    if not (np.all(d["slot"] >= 0) and np.all(d["slot"] < M)): bad.append("slot 0 to M - 1")
    return bad
def reference(x, slot, w):
    h = np.arange(8)
    v = np.ascontiguousarray(x.astype(np.float32).astype(np.int64).reshape(N, 8, 16, S).transpose(0, 3, 1, 2)).reshape(N * S, 8, 16)
    s = slot.transpose(0, 2, 1).reshape(N * S, 8)
    c = w.astype(np.int64).reshape(N, 1, 8, 16)
    for layer in range(2):
        if layer == 1: s = np.sum(v.reshape(N, S, 8, 16) * c, axis=3).reshape(N * S, 8) & (M - 1)
        m = np.full((8, M, 16), -256, np.int64); y = np.empty_like(v)
        for t in range(N * S):
            y[t] = np.maximum(m[h, s[t]], v[t]); m[h, s[t]] = y[t]
        v = y
    return {"y": np.ascontiguousarray(v.reshape(N, S, 8, 16).transpose(0, 2, 3, 1)).reshape(N, 128, S).astype(np.float32).astype(BF)}

@@ -1,0 +1,381 @@
+from concourse.bass import DstId, RemoteDMATransfer
+from concourse.mybir import AluOpType, ActivationFunctionType, AxisListType
+
+S = 1024
+M = 512
+H = M // 2
+NR = 8
+SL = 64
+W = S + H
+WP = 1040
+K = S // 16
+
+F32, BF, F16, I32, U16 = "float32", "bfloat16", "float16", "int32", "uint16"
+SCRATCH = {"ci": ("sbuf", [128, 8, 16], I32), "cf": ("sbuf", [128, 8, 16], F16), "ex": ("sbuf", [128, 8, 128], F16)}
+for _name, _cols, _dt in (
+        ("pci", 8, I32), ("ai", 8, I32), ("col", 16, F32), ("ws", 8, F32), ("cc", 144, F32), ("t1", M, BF),
+        ("t2", M, BF), ("tab1", M, BF), ("tab2", M, BF), ("gm", 8, F32), ("z", 144, BF), ("zq", 144, BF),
+        ("zd", 144, F16), ("z2", 80, BF), ("bk", 128, F32), ("trs", 128, F32), ("tri", 128, F32), ("trq", 128, F32),
+        ("idf", 128, F32), ("i5", 128, BF), ("sw", 128, BF), ("swb", 128, BF), ("i32", 32, F32), ("nc", 32, F32),
+        ("lows", H, BF), ("c16", H, F32), ("rs", W, BF)):
+    SCRATCH[_name] = ("sbuf", [128, _cols], _dt)
+STREAM = (("xs", S, BF), ("yl", S, BF), ("zw", 144, BF), ("hi", K, I32), ("hm", K, I32), ("s16", K, F16), ("l1", K, U16),
+          ("l2", K, U16), ("sl", 16, U16), ("se", 32, F32), ("he", 32, U16), ("tot", 8, F32), ("m1", S, BF),
+          ("cum", S, F16), ("pra", S, F16), ("prb", S, F16), ("mh", S, F32), ("wb", WP, F32), ("cw", WP, F32),
+          ("yw", 2 * W, BF), ("tb", M, BF), ("su", M, BF), ("pt", M, BF))
+for _s in "01":
+    for _name, _cols, _dt in STREAM:
+        SCRATCH[_name + _s] = ("sbuf", [128, _cols], _dt)
+    for _name in ("pa", "pb", "pc", "pd"):
+        SCRATCH[_name + _s] = ("psum", [128, 512], F32)
+    for _l in "01":
+        for _name, _cols, _dt in (("yo", S, BF), ("ls", K, U16), ("xw", 2 * W, BF), ("ck", H, BF), ("la", NR * SL, BF),
+                                  ("rz", W, BF if _s + _l == "01" else F32), ("lb", 3 * H, BF), ("pf", NR * SL, BF),
+                                  ("pl", H, BF)):
+            SCRATCH[_name + _s + _l] = ("sbuf", [128, _cols], _dt)
+SEMAPHORES = ["cV", "cA", "cP", "cG", "sent"] + \
+    [a + s + h for a in ("dslot", "dx", "dw", "up", "down") for s in "01" for h in "01"] + \
+    ["st" + s + h + j for s in "01" for h in "01" for j in "01"]
+
+OP = AluOpType
+AF = ActivationFunctionType
+
+ORDER = """
+S:ci00.1 S:ci10.1 A:ci01.1 A:ci11.1 S:xs00.1 S:xs01.1 S:xs10.1 S:xs11.1 S:ws00.1 S:ws01.1 S:ws10.1 S:ws11.1
+V:xw00.1 G:pci.1 V:pf.1 G:cc.1 A:wb0.1 A:wb1.1 V:ai.1 V:idf.1 V:af.1 V:b256.1 V:g16.1 V:i5.1 V:ps.1 V:bk.1 V:gm.1
+V:a4.1 V:z.1 V:z2.1 V:cf.1 V:ex3.1 V:ex2.1 V:ex7.1 V:ex5.1 V:ex0.1 V:ex4.1 V:ex6.1 V:ex1.1 G:t1.1 G:t2.1 V:c11.1
+V:tab1.1 P:pa0.1 V:hi0.1 P:pa1.1 V:hi1.1 V:hm0.1 V:hm1.1 V:ls00.1 A:m10.1 V:tab2.1 V:ls10.1 A:m11.1 V:s161.1
+V:mh0.1 G:trs.1 G:tri.1 G:c16.1 P:pa0.2 V:cum0.1 V:cd.1 V:pra0.1 V:totb0.1 P:pa0.3 V:l10.1 A:wb0.2 P:pa1.2
+V:cum1.1 V:s160.1 V:pra1.1 P:pa1.3 V:zd.1 P:pc0.1 P:pc0.2 V:trq.1 V:mh1.1 V:l11.1 P:pc0.3 V:sl0.1 A:wb1.2
+V:totb1.1 V:cw0.1 V:zq.1 V:prb0.1 P:pb0.1 V:c5.1 G:i32.1 V:nc.1 V:swb.1 V:sw.1 V:se0.1 V:low.1 P:pb0.2 V:l20.1
+V:he0.1 G:rz00.1 A:rz00.1 A:rs.1 G:xw10.1 P:pc1.1 P:pc1.2 P:pc1.3 V:xsc00.1 V:xsc00.2 V:sl1.1 V:ywb0.1 A:tbb0.1
+swv00.1 P:pb0.3 P:pb1.1 V:ywa0.1 A:tba0.1 V:cw1.1 V:ck00.1 V:prb1.1 G:xwa10.1 V:se1.1 V:lao00.1 V:he1.1 G:rz10.1
+P:pb1.2 V:l21.1 V:xsc10.1 V:xsc10.2 sendup00.1 sendlow00.1 G:xwa01.1 V:la00.1 pf00.1 pf00.2 pf00.3 pf00.4 V:zw0.1
+pf00.5 P:pb0.4 A:rz10.1 A:rs.2 A:su0.1 A:yl0.1 V:ywb1.1 A:tbb1.1 P:pb1.3 swv10.1 V:ywa1.1 A:tba1.1 P:pb1.4
+A:su1.1 A:yl1.1 V:lb00.1 pm00.1 senddown00.1 V:ck10.1 sendup10.1 sendlow10.1 G:xw01.1 pm00.2 V:pl00.1 V:pta0.1
+P:pd0.1 V:ptb0.1 V:lao10.1 V:yo00_0.1 P:pa0.4 V:hi0.2 V:hm0.2 V:ls01.1 A:m10.2 V:la10.1 pf10.1 pf10.2 V:s160.2
+pf10.3 pf10.4 pf10.5 senddown10.1 G:lows.1 G:rz01.1 G:xwa11.1 G:xw11.1 G:rz11.1 P:pa0.5 V:cum0.2 V:zw1.1
+V:pra0.2 V:lb10.1 pm10.1 P:pc0.4 P:pa0.6 P:pc0.5 A:mh0.1 V:l10.2 A:wb0.3 pm10.2 V:pl10.1 P:pc0.6 P:pd1.1
+V:pta1.1 V:ptb1.1 V:yo10_0.1 P:pa1.4 V:hi1.2 V:sl0.2 V:hm1.2 V:ls11.1 A:m11.2 P:pa1.5 V:cw0.2 V:s161.2 V:se0.2
+V:prb0.2 P:pb0.5 P:pb0.6 V:cum1.2 V:he0.2 V:pra1.2 P:pc1.4 P:pc1.5 P:pa1.6 V:rz01.1 V:l20.2 V:l11.2 A:mh1.1
+P:pc1.6 V:xsc01.1 V:sl1.2 V:xsc01.2 A:wb1.3 V:cw1.2 V:ywb0.2 A:tbb0.2 swv01.1 V:ywa0.2 V:prb1.2 P:pb0.7
+A:tba0.2 P:pb0.8 V:ck01.1 sendup01.1 sendlow01.1 P:pb1.5 P:pb1.6 V:se1.2 V:he1.2 V:lao01.1 A:rz11.1 A:rs.3
+V:l21.2 V:xsc11.1 V:xsc11.2 V:ywb1.2 A:tbb1.2 P:pb1.7 V:la01.1 pf01.1 pf01.2 pf01.3 pf01.4 pf01.5 senddown01.1
+V:ywa1.2 A:tba1.2 swv11.1 V:ck11.1 sendup11.1 sendlow11.1 V:lb01.1 pm01.1 pm01.2 V:pl01.1 P:pb1.8 P:pd0.2
+A:su0.2 V:ptb0.2 V:pta0.2 V:lao11.1 A:yl0.2 V:yo01_0.1 S:out000.1 V:la11.1 pf11.1 pf11.2 pf11.3 pf11.4 pf11.5
+senddown11.1 V:yo01_1.1 S:out001.1 A:yl1.2 A:su1.2 A:out010.1 A:out011.1 V:lb11.1 pm11.1 pm11.2 V:pl11.1
+V:pta1.2 P:pd1.2 V:ptb1.2 V:yo11_0.1 S:out100.1 A:out110.1 V:yo11_1.1 A:out111.1 S:out101.1 end.1
+"""
+
+
+def needs(ops):
+    writer, readers, res = {}, {}, []
+    for n, o in enumerate(ops):
+        deps = set()
+        for k in o["r"] + o["w"]:
+            if k in writer:
+                deps.add(writer[k])
+        for k in o["w"]:
+            deps.update(readers.get(k, []))
+        res.append(deps)
+        if o["kind"] != "remote":
+            for k in o["r"]:
+                readers.setdefault(k, []).append(n)
+        for k in o["w"]:
+            writer[k] = n
+            readers[k] = []
+    return res
+
+
+def emit(g, T, ops):
+    queue = {"V": g.vector, "A": g.scalar, "P": g.tensor, "G": g, "S": g.sync}
+    waited, need = {}, []
+    for o, deps in zip(ops, needs(ops)):
+        last = {}
+        for d in deps:
+            p = ops[d]
+            if p["e"] == "P" and o["e"] == "P" and p["sem"] is None:
+                continue
+            key = p["sem"] if p["sem"] is not None else p["e"]
+            last[key] = max(last.get(key, -1), d)
+        mine = []
+        for key in sorted(last):
+            d = last[key]
+            if waited.get((o["e"], key), -1) < d:
+                waited[(o["e"], key)] = d
+                ops[d]["sig"] = True
+                mine.append(d)
+        need.append(mine)
+    count = {"V": 0, "A": 0, "P": 0, "G": 0}
+    for o, mine in zip(ops, need):
+        for d in mine:
+            p = ops[d]
+            queue[o["e"]].wait_ge(T.sem[p["sem"] if p["sem"] is not None else "c" + p["e"]], p["val"])
+        if o["fn"] is None:
+            continue
+        ins = o["fn"]()
+        if o["kind"] == "dma":
+            ins.then_inc(T.sem[o["sem"]], 16)
+        elif o["kind"] == "compute" and o["sig"]:
+            count[o["e"]] += 1
+            o["val"] = count[o["e"]]
+            ins.then_inc(T.sem["c" + o["e"]], 1)
+
+
+def build(g, core, T, topo, rank):
+    ops, sent, seen = [], [0], {}
+    V, A, P = g.vector, g.scalar, g.tensor
+
+    def rec(e, fn, r, w, kind="compute", sem=None, val=0, tag=None):
+        tag = tag if tag is not None else e + ":" + w[-1]
+        seen[tag] = seen.get(tag, 0) + 1
+        ops.append({"e": e, "fn": fn, "r": list(r), "w": list(w), "kind": kind, "sem": sem, "val": val,
+                    "sig": False, "tag": tag + "." + str(seen[tag])})
+
+    def dma(e, out, in_, r, w, sem):
+        q = g.sync if e == "S" else A
+        rec(e, lambda: q.dma_start(out, in_), r, w, kind="dma", sem=sem, val=16)
+
+    def ts(out, in0, s1, s2, op0, op1, r, w):
+        if op1 is None:
+            rec("V", lambda: V.tensor_scalar(out, in0, s1, None, op0), r, w)
+        else:
+            rec("V", lambda: V.tensor_scalar(out, in0, s1, s2, op0, op1), r, w)
+
+    def cp(out, in_, r, w):
+        rec("V", lambda: V.tensor_copy(out, in_), r, w)
+
+    def tt(out, a, b, op, r, w, tag=None):
+        rec("V", lambda: V.tensor_tensor(out, a, b, op), r, w, tag=tag)
+
+    def scan(out, d0, d1, init, op0, op1, r, w):
+        rec("V", lambda: V.tensor_tensor_scan(out, d0, d1, init, op0, op1), r, w)
+
+    def act(out, in_, r, w, func=AF.Identity, **kw):
+        rec("A", lambda: A.activation(out, in_, func, **kw), r, w)
+
+    def iota(out, pattern, base, mult, w, whole=False):
+        if whole:
+            rec("G", lambda: g.iota(out, pattern, base, mult), [], w)
+        else:
+            rec("G", lambda: g.iota(out, pattern, base, mult, allow_small_or_imprecise_dtypes=True), [], w)
+
+    def fill(buf, lo, hi, value, w):
+        iota(buf[:, lo:hi], [[0, hi - lo]], value, 0, w)
+
+    def mm(items, r, w, first=True, final=True, tag=None):
+        def fn():
+            ins = None
+            for n, (out, lhsT, rhs) in enumerate(items):
+                ins = P.matmul(out, lhsT, rhs, first and n == 0, final and n == len(items) - 1)
+            return ins
+        rec("P", fn, r, w, tag=tag)
+
+    def wrap(bank, zz, src):
+        return [(bank[:, 0:K], zz[:, 15 - i:143 - i], src[:, i:S:16]) for i in range(16)]
+
+    def send(pairs, width, sem, r, tag):
+        transfers = []
+        for n, (dst_rank, src, dst) in enumerate(pairs):
+            c = T.cores[dst_rank]
+            rid, pid = topo.addr(c)[0], topo.addr(c)[1]
+            eng = topo.engines(core, c)[n * width:(n + 1) * width]
+            transfers.append(RemoteDMATransfer(dst_ids=[DstId(rid=rid, pnc=pid)],
+                                               dma_engine_mask=sum(1 << e for e in eng),
+                                               remote_sem=T.sem[sem], src=src, dst=dst))
+        sent[0] += width * len(pairs)
+        rec("G", lambda: g.remote_dma_fused(transfers, local_sem=T.sem.sent), r, [], kind="remote", tag=tag)
+
+    pf, af, g16, a4, c11, c5, cd, b256, low, ps = (T.col[:, j:j + 1] for j in range(10))
+
+    cik = ["ci00", "ci01", "ci10", "ci11"]
+    for s in range(2):
+        for h in range(2):
+            dma("SA"[h], T.ci[64 * h:64 * h + 64, 4 * s:4 * s + 4, :], T.slot[4 * s:4 * s + 4, S * h:S * h + S],
+                [], ["ci%d%d" % (s, h)], "dslot%d%d" % (s, h))
+    for s in range(2):
+        for h in range(2):
+            dma("S", T["xs%d" % s][64 * h:64 * h + 64, :], T.x[64 * s:64 * s + 64, S * h:S * h + S],
+                cik, ["xs%d%d" % (s, h)], "dx%d%d" % (s, h))
+    for s in range(2):
+        for h in range(2):
+            dma("S", T.ws[64 * h:64 * h + 64, 4 * s:4 * s + 1], T.w[64 * s:64 * s + 64, :],
+                [], ["ws%d%d" % (s, h)], "dw%d%d" % (s, h))
+    rec("V", lambda: V.memset(T.xw00[:], -256.0), [], ["xwa00", "xw00"])
+    iota(T.pci[:, 0:1], [[0, 1]], 0, 1, ["pci"], whole=True)
+    iota(T.cc[:], [[1, 144]], 0, 0, ["cc"])
+    iota(T.t1[:], [[0, 2], [1, 16], [0, 16]], 0, 0, ["t1"])
+    for s in "01":
+        act(T["wb" + s][:, 0:16], T.cc[:, 0:16], ["cc"], ["wb" + s], func=AF.Tanh, scale=0.0)
+    ts(T.ai[:, 0:1], T.pci[:, 0:1], 15, None, OP.bitwise_and, None, ["pci"], ["ai"])
+    cp(pf, T.pci[:, 0:1], ["pci"], ["pf"])
+    cp(af, T.ai[:, 0:1], ["ai"], ["af"])
+    ts(g16, pf, af, None, OP.subtract, None, ["pf", "af"], ["g16"])
+    ts(a4, af, 4.0, None, OP.mult, None, ["af"], ["a4"])
+    ts(b256, pf, 64.0, 256.0, OP.is_ge, OP.mult, ["pf"], ["b256"])
+    ts(T.bk[:], T.cc[:, 0:128], g16, 15.0, OP.subtract, OP.is_le, ["cc", "g16"], ["bk"])
+    ts(T.gm[:], T.cc[:, 0:128:16], g16, None, OP.is_equal, None, ["cc", "g16"], ["gm"])
+    ts(T.z2[:], T.cc[:, 0:80], a4, 3.0, OP.subtract, OP.is_equal, ["cc", "a4"], ["z2"])
+    ts(T.z[:], T.cc[:], g16, 15.0, OP.subtract, OP.is_equal, ["cc", "g16"], ["z"])
+    ts(T.tab1[:], T.t1[:], af, None, OP.is_equal, None, ["t1", "af"], ["tab1"])
+    rec("G", lambda: g.affine_select(T.trs[:], T.bk[:], [[1, 128]], OP.is_gt, 0.0, 0, -1), ["bk"], ["trs"])
+    iota(T.t2[:], [[0, 32], [1, 16]], 0, 0, ["t2"])
+    rec("G", lambda: g.affine_select(T.tri[:], T.bk[:], [[1, 128]], OP.is_ge, 0.0, 0, -1), ["bk"], ["tri"])
+    iota(T.i32[:], [[0, 2], [1, 16]], 0, 0, ["i32"])
+    fill(T.lows, 0, H, -256, ["lows"])
+    fill(T.c16, 0, H, 16, ["c16"])
+    fill(T.rz00, 0, W, 0, ["rz00"])
+    cp(T.cf[:], T.ci[:], cik, ["cf"])
+    for h in range(8):
+        ts(T.ex[:, :, 16 * h:16 * h + 16], T.cf[:], T.gm[:, h:h + 1], None, OP.mult, None, ["cf", "gm"], ["ex%d" % h])
+    for s in range(2):
+        mm([(T["pa%d" % s][:, 0:K], T.ex[:, 4 * s + b, :], T.z2[:, 3 - b:3 - b + K]) for b in range(4)],
+           ["ex%d" % h for h in range(8)] + ["z2"], ["pa%d" % s])
+    ts(T.tab2[:], T.t2[:], af, None, OP.is_equal, None, ["t2", "af"], ["tab2"])
+    ts(cd, af, -79.0, None, OP.mult, None, ["af"], ["cd"])
+    ts(c11, af, 11.0, None, OP.mult, None, ["af"], ["c11"])
+    ts(c5, af, 5.0, 0.25, OP.mult, OP.add, ["af"], ["c5"])
+    ts(low, b256, -256.0, None, OP.add, None, ["b256"], ["low"])
+    ts(ps, b256, -0.5, pf, OP.mult, OP.add, ["b256", "pf"], ["ps"])
+    ts(T.zd[:], T.z[:], cd, None, OP.mult, None, ["z", "cd"], ["zd"])
+    ts(T.i5[:], T.cc[:, 0:128], pf, 5.0, OP.is_equal, OP.mult, ["cc", "pf"], ["i5"])
+    ts(T.idf[:], T.cc[:, 0:128], pf, None, OP.is_equal, None, ["cc", "pf"], ["idf"])
+    ts(T.trq[:], T.trs[:], 0.0625, None, OP.mult, None, ["trs"], ["trq"])
+    ts(T.zq[:], T.z[:], 0.0625, None, OP.mult, None, ["z"], ["zq"])
+    ts(T.nc[:], T.i32[:], c5, None, OP.add, None, ["i32", "c5"], ["nc"])
+    ts(T.sw[:], T.cc[:, 0:128], ps, 64.0, OP.subtract, OP.is_equal, ["cc", "ps"], ["sw"])
+    ts(T.swb[:], T.cc[:, 0:128], pf, 64.0, OP.subtract, OP.is_equal, ["cc", "pf"], ["swb"])
+    for s in range(2):
+        ts(T["zw%d" % s][:], T.z[:], T.ws[:, 4 * s:4 * s + 1], None, OP.mult, None,
+           ["z", "ws%d0" % s, "ws%d1" % s], ["zw%d" % s])
+    for n in ("10", "01", "11"):
+        fill(T["xw" + n], 0, W, -256, ["xwa" + n])
+        fill(T["xw" + n], W, 2 * W, -256, ["xw" + n])
+        fill(T["rz" + n], 0, W, 256 if n == "01" else 0, ["rz" + n])
+
+    def layer(st, L):
+        s, n = str(st), "%d%d" % (st, L)
+        b = {x[0]: T[x[0] + s] for x in STREAM}
+        ls, xw, rz, ck, la, lb, pfx, pl, yo = (T[x + n] for x in ("ls", "xw", "rz", "ck", "la", "lb", "pf", "pl", "yo"))
+        pa, pb, pc, pd, tot, m1, mh, cw, yw, tb, he = (T[x + s] for x in ("pa", "pb", "pc", "pd", "tot", "m1", "mh",
+                                                                          "cw", "yw", "tb", "he"))
+
+        def k(*names):
+            return [x + s for x in names]
+        ts(b["hi"][:], pa[:, 0:K], b256, None, OP.add, None, ["b256"], k("pa", "hi"))
+        ts(b["hm"][:], b["hi"][:], M - 1, None, OP.bitwise_and, None, k("hi"), k("hm"))
+        cp(ls[:], b["hm"][:], k("hm"), ["ls" + n])
+        cp(b["s16"][:], b["hm"][:], k("hm"), k("s16"))
+        act(m1[:], T.tab1[:].indirect(ls[:]), ["tab1", "ls" + n], k("tota", "m1"), accum_out=tot[:, 0:1])
+        mm([(pa[:, 0:1], T.trs[:], tot[:, 0:1])], ["trs"] + k("tota"), k("pa"))
+        mm([(pc[:, 0:1], T.trs[:], tot[:, 0:1])], k("tota"), k("pc"))
+        mm([(pc[:, 1:2], T.tri[:], tot[:, 0:1])], ["tri"] + k("tota"), k("pc"))
+        if L == 0:
+            ts(mh[:], T.tab2[:].indirect(ls[:]), 16.0, None, OP.mult, None, ["tab2", "ls" + n], k("mh"))
+            rec("V", lambda: V.tensor_reduce(tot[:, 4:5], mh[:], AxisListType.X, OP.add), k("mh"), k("totb"))
+        else:
+            act(mh[:], T.tab2[:].indirect(ls[:]), ["tab2", "ls" + n], k("totb", "mh"), scale=16.0,
+                accum_out=tot[:, 4:5])
+        scan(b["cum"][:], m1[:], m1[:], pa[:, 0:1], OP.add, OP.max, k("m1"), k("pa", "cum"))
+        scan(b["pra"][:], b["cum"][:], m1[:], 0.0, OP.max, OP.mult, k("cum", "m1"), k("pra"))
+        mm(wrap(pa, T.z, b["pra"]), ["z"] + k("pra"), k("pa"))
+        cp(b["l1"][:], pa[:, 0:K], [], k("pa", "l1"))
+        act(b["wb"][:, 0:S + 1].indirect(b["l1"][:]), mh[:], k("mh", "l1"), k("wb"), func=AF.Tanh)
+        mm([(pc[:, 2:3], T.idf[:], c11), (pc[:, 2:3], T.trq[:], tot[:, 4:5])], ["idf", "c11", "trq"] + k("totb"),
+           k("pc"))
+        mm([(pb[:, 0:K], T.i5[:], b["s16"][:])] + wrap(pb, T.zd, m1), ["i5", "zd"] + k("s16", "m1"), k("pb"),
+           final=False)
+        cp(b["sl"][:, 0:2], pc[:, 0:2], [], k("pc", "sl"))
+        scan(cw[:, 0:S + 1], b["wb"][:, 0:S + 1], b["wb"][:, 0:S + 1], pc[:, 2:3], OP.add, OP.max,
+             k("wb"), k("pc", "cw"))
+        cwin = cw[:, 0:S + 1]
+        tt(b["prb"][:], cwin.indirect(b["l1"][:]), mh[:], OP.mult, k("cw", "l1", "mh"), k("prb"))
+        mm(wrap(pb, T.zq, b["prb"]), ["zq"] + k("prb"), k("pb"), first=False)
+        tt(b["se"][:], cwin.indirect(b["sl"][:, 0:2]), T.nc[:], OP.add, ["nc"] + k("cw", "sl"), k("se"))
+        cp(he[:], b["se"][:], k("se"), k("he"))
+        ts(b["l2"][:], pb[:, 0:K], 0.25, None, OP.add, None, [], k("pb", "l2"))
+        if n == "01":
+            cp(rz[:].indirect(he[:, 0:16]), T.lows[:], ["lows"] + k("he"), ["rz" + n])
+            cap, capk = rz, "rz" + n
+        else:
+            act(rz[:].indirect(he[:, 0:16]), T.c16[:], ["c16"] + k("he"), ["rz" + n], func=AF.Tanh)
+            act(T.rs[:], rz[:], ["rz" + n], ["rs"], scale=-1024.0, bias=512.0)
+            cap, capk = T.rs, "rs"
+        src, srck = (b["xs"], ["xs%s0" % s, "xs%s1" % s]) if L == 0 else (T["yo%s0" % s], ["yo%s0_0" % s])
+        for j in range(2):
+            cp(xw[:].indirect(b["l2"][:, 32 * j:32 * j + 32]), src[:, 512 * j:512 * j + 512], srck + k("l2"),
+               ["xwa" + n, "xw" + n, "xsc" + n])
+        scan(yw[:, W:2 * W], cap[:], xw[:, W:2 * W], -256.0, OP.min, OP.max, ["xw" + n, capk], k("ywb"))
+        scan(yw[:, 0:W], cap[:], xw[:, 0:W], -256.0, OP.min, OP.max, ["xw" + n, capk], k("ywa"))
+        act(tb[:, H:M], yw[:, W:2 * W].indirect(he[:, 16:32]), k("ywb", "he"), k("tbb"))
+        act(tb[:, 0:H], yw[:, 0:W].indirect(he[:, 16:32]), k("ywa", "he"), k("tba"))
+        owners, upper = list(range(NR // 2)), list(range(NR // 2, NR))
+        if rank < NR - 1:
+            mm([(pa[:, 0:H], T.sw[:], tb[:, H:M])], ["sw"] + k("tbb"), k("pa"), tag="swv" + n)
+            tt(ck[:], tb[:, 0:H], pa[:, 0:H], OP.max, k("tba"), ["pa" + s, "ck" + n])
+            send([(o, ck[:, SL * o:SL * o + SL], la[:, SL * rank:SL * rank + SL]) for o in owners if o != rank], 2,
+                 "up" + n, ["ck" + n], "sendup" + n)
+        if rank < NR // 2 - 1:
+            send([(r, ck[:], lb[:, H * rank:H * rank + H]) for r in range(rank + 1, NR // 2)], 2, "down" + n,
+                 ["ck" + n], "sendlow" + n)
+        mm([(pb[:, 0:H], T.swb[:], tb[:, H:M])], ["swb"] + k("tbb"), k("pb"))
+        mm([(pb[:, H:M], T.swb[:], tb[:, 0:H])], k("tba"), k("pb"))
+        act(b["su"][:], pb[:], ["low"], k("pb", "su"), bias=low)
+        act(b["yl"][:], yw[:].indirect(b["l2"][:]), k("ywa", "ywb", "l2"), k("yl"))
+        below, bk = pl[:], ["pl" + n]
+        if rank in owners:
+            own = slice(SL * rank, SL * rank + SL)
+            cp(la[:, own], ck[:, own], ["ck" + n], ["lao" + n])
+            rec("V", None, [], ["la" + n], kind="arrival", sem="up" + n, val=2 * (NR - 2))
+            tt(pfx[:, 0:2 * SL], la[:, 0:2 * SL], la[:, 2 * SL:4 * SL], OP.max, ["la" + n, "lao" + n], ["pfp" + n],
+               tag="pf" + n)
+            x0, x1, key = pfx[:, 0:SL], pfx[:, SL:2 * SL], "pfp" + n
+            for r in upper:
+                tt(pfx[:, SL * r:SL * r + SL], x0, x1, OP.max, [key], ["pf%s_%d" % (n, r)], tag="pf" + n)
+                x0, x1, key = pfx[:, SL * r:SL * r + SL], la[:, SL * r:SL * r + SL], "pf%s_%d" % (n, r)
+            send([(r, pfx[:, SL * r:SL * r + SL], pl[:, own]) for r in upper], 2, "down" + n,
+                 ["pf%s_%d" % (n, r) for r in upper], "senddown" + n)
+            if rank > 0:
+                rec("V", None, [], ["lb" + n], kind="arrival", sem="down" + n, val=2 * rank)
+                below, bk = lb[:, 0:H], ["lb" + n]
+                for r in range(1, rank):
+                    tt(pl[:], below, lb[:, H * r:H * r + H], OP.max, bk + ["lb" + n], ["pl" + n], tag="pm" + n)
+                    below, bk = pl[:], ["pl" + n]
+        else:
+            rec("V", None, [], ["pl" + n], kind="arrival", sem="down" + n, val=2 * len(owners))
+        table, tk = b["su"], k("su")
+        if rank > 0:
+            mm([(pd[:, 0:H], T.sw[:], below)], ["sw"] + bk, k("pd"))
+            tt(b["pt"][:, 0:H], below, b["su"][:, 0:H], OP.max, bk + k("su"), k("pta"))
+            tt(b["pt"][:, H:M], b["su"][:, H:M], pd[:, 0:H], OP.max, k("su"), k("pd", "ptb"))
+            table, tk = b["pt"], k("pta", "ptb")
+        cuts = [0, S] if L == 0 else [0, 640, S]
+        for j in range(len(cuts) - 1):
+            lo, hi = cuts[j], cuts[j + 1]
+            key = "yo%s_%d" % (n, j)
+            tt(yo[:, lo:hi], table[:].indirect(ls[:, lo // 16:hi // 16]), b["yl"][:, lo:hi], OP.max,
+               tk + ["ls" + n] + k("yl"), [key])
+            if L == 1:
+                for h in range(2):
+                    dma("SA"[h], T.y[64 * st:64 * st + 64, S * h + lo:S * h + hi], yo[64 * h:64 * h + 64, lo:hi],
+                        [key], ["out%d%d%d" % (st, h, j)], "st%d%d%d" % (st, h, j))
+        if L == 0:
+            mm(wrap(pa, b["zw"], yo), ["yo%s_0" % n] + k("zw"), k("pa"))
+
+    for L in range(2):
+        for st in range(2):
+            layer(st, L)
+    rec("S", None, ["out%d%d%d" % (st, h, j) for st in range(2) for h in range(2) for j in range(2)], [],
+        kind="end", tag="end")
+    return ops, sent[0]
+
+
+def rank_program(g, core, T, topo):
+    rank = T.rank_of(core)
+    if rank is None:
+        return
+    ops, sent = build(g, core, T, topo, rank)
+    place = {t: n for n, t in enumerate(ORDER.split())}
+    ops.sort(key=lambda o: place[o["tag"]])
+    emit(g, T, ops)
+    g.wait_ge(T.sem.sent, sent)

@@ -17,7 +17,7 @@ for _name, _cols, _dt in (
         ("t2", M, BF), ("tab1", M, BF), ("tab2", M, BF), ("gm", 8, F32), ("z", 144, BF), ("zq", 144, BF),
         ("zd", 144, F16), ("z2", 80, BF), ("bk", 128, F32), ("trs", 128, F32), ("tri", 128, F32), ("trq", 128, F32),
         ("idf", 128, F32), ("i5", 128, BF), ("sw", 128, BF), ("swb", 128, BF), ("i32", 32, F32), ("nc", 32, F32),
-        ("lows", H, BF), ("c16", H, F32), ("rs", W, BF)):
+        ("lows", H, BF), ("c16", H, F32), ("rs", W, BF), ("ga", 512, BF), ("wc", WP, F32), ("wa", WP, F32)):
     SCRATCH[_name] = ("sbuf", [128, _cols], _dt)
 STREAM = (("xs", S, BF), ("yl", S, BF), ("zw", 144, BF), ("hi", K, I32), ("hm", K, I32), ("s16", K, F16), ("l1", K, U16),
           ("l2", K, U16), ("sl", 16, U16), ("se", 32, F32), ("he", 32, U16), ("tot", 8, F32), ("m1", S, BF),
@@ -45,26 +45,27 @@ S:ci00.1 S:ci10.1 A:ci01.1 A:ci11.1 S:xs00.1 S:xs01.1 S:xs10.1 S:xs11.1 S:ws00.1
 V:xw00.1 G:pci.1 V:pf.1 G:cc.1 A:wb0.1 A:wb1.1 V:ai.1 V:idf.1 V:af.1 V:b256.1 V:g16.1 V:i5.1 V:ps.1 V:bk.1 V:gm.1
 V:a4.1 V:z.1 V:z2.1 V:cf.1 V:ex3.1 V:ex2.1 V:ex7.1 V:ex5.1 V:ex0.1 V:ex4.1 V:ex6.1 V:ex1.1 G:t1.1 G:t2.1 V:c11.1
 V:tab1.1 P:pa0.1 V:hi0.1 P:pa1.1 V:hi1.1 V:hm0.1 V:hm1.1 V:ls00.1 A:m10.1 V:tab2.1 V:ls10.1 A:m11.1 V:s161.1
-V:mh0.1 G:trs.1 G:tri.1 G:c16.1 P:pa0.2 V:cum0.1 V:cd.1 V:pra0.1 V:totb0.1 P:pa0.3 V:l10.1 A:wb0.2 P:pa1.2
-V:cum1.1 V:s160.1 V:pra1.1 P:pa1.3 V:zd.1 P:pc0.1 P:pc0.2 V:trq.1 V:mh1.1 V:l11.1 P:pc0.3 V:sl0.1 A:wb1.2
-V:totb1.1 V:cw0.1 V:zq.1 V:prb0.1 P:pb0.1 V:c5.1 G:i32.1 V:nc.1 V:swb.1 V:sw.1 V:se0.1 V:low.1 P:pb0.2 V:l20.1
-V:he0.1 G:rz00.1 A:rz00.1 A:rs.1 G:xw10.1 P:pc1.1 P:pc1.2 P:pc1.3 V:xsc00.1 V:xsc00.2 V:sl1.1 V:ywb0.1 A:tbb0.1
-swv00.1 P:pb0.3 P:pb1.1 V:ywa0.1 A:tba0.1 V:cw1.1 V:ck00.1 V:prb1.1 G:xwa10.1 V:se1.1 V:lao00.1 V:he1.1 G:rz10.1
-P:pb1.2 V:l21.1 V:xsc10.1 V:xsc10.2 sendup00.1 sendlow00.1 G:xwa01.1 V:la00.1 pf00.1 pf00.2 pf00.3 pf00.4 V:zw0.1
-pf00.5 P:pb0.4 A:rz10.1 A:rs.2 A:su0.1 A:yl0.1 V:ywb1.1 A:tbb1.1 P:pb1.3 swv10.1 V:ywa1.1 A:tba1.1 P:pb1.4
-A:su1.1 A:yl1.1 V:lb00.1 pm00.1 senddown00.1 V:ck10.1 sendup10.1 sendlow10.1 G:xw01.1 pm00.2 V:pl00.1 V:pta0.1
-P:pd0.1 V:ptb0.1 V:lao10.1 V:yo00_0.1 P:pa0.4 V:hi0.2 V:hm0.2 V:ls01.1 A:m10.2 V:la10.1 pf10.1 pf10.2 V:s160.2
-pf10.3 pf10.4 pf10.5 senddown10.1 G:lows.1 G:rz01.1 G:xwa11.1 G:xw11.1 G:rz11.1 P:pa0.5 V:cum0.2 V:zw1.1
-V:pra0.2 V:lb10.1 pm10.1 P:pc0.4 P:pa0.6 P:pc0.5 A:mh0.1 V:l10.2 A:wb0.3 pm10.2 V:pl10.1 P:pc0.6 P:pd1.1
-V:pta1.1 V:ptb1.1 V:yo10_0.1 P:pa1.4 V:hi1.2 V:sl0.2 V:hm1.2 V:ls11.1 A:m11.2 P:pa1.5 V:cw0.2 V:s161.2 V:se0.2
-V:prb0.2 P:pb0.5 P:pb0.6 V:cum1.2 V:he0.2 V:pra1.2 P:pc1.4 P:pc1.5 P:pa1.6 V:rz01.1 V:l20.2 V:l11.2 A:mh1.1
-P:pc1.6 V:xsc01.1 V:sl1.2 V:xsc01.2 A:wb1.3 V:cw1.2 V:ywb0.2 A:tbb0.2 swv01.1 V:ywa0.2 V:prb1.2 P:pb0.7
-A:tba0.2 P:pb0.8 V:ck01.1 sendup01.1 sendlow01.1 P:pb1.5 P:pb1.6 V:se1.2 V:he1.2 V:lao01.1 A:rz11.1 A:rs.3
-V:l21.2 V:xsc11.1 V:xsc11.2 V:ywb1.2 A:tbb1.2 P:pb1.7 V:la01.1 pf01.1 pf01.2 pf01.3 pf01.4 pf01.5 senddown01.1
-V:ywa1.2 A:tba1.2 swv11.1 V:ck11.1 sendup11.1 sendlow11.1 V:lb01.1 pm01.1 pm01.2 V:pl01.1 P:pb1.8 P:pd0.2
-A:su0.2 V:ptb0.2 V:pta0.2 V:lao11.1 A:yl0.2 V:yo01_0.1 S:out000.1 V:la11.1 pf11.1 pf11.2 pf11.3 pf11.4 pf11.5
-senddown11.1 V:yo01_1.1 S:out001.1 A:yl1.2 A:su1.2 A:out010.1 A:out011.1 V:lb11.1 pm11.1 pm11.2 V:pl11.1
-V:pta1.2 P:pd1.2 V:ptb1.2 V:yo11_0.1 S:out100.1 A:out110.1 V:yo11_1.1 A:out111.1 S:out101.1 end.1
+V:mh0.1 G:trs.1 G:i32.1 G:tri.1 G:c16.1 G:rz00.1 G:xwa10.1 G:rz10.1 G:xw10.1 G:wc.1 G:lows.1 P:pa0.2 P:pc0.1
+V:cum0.1 V:cd.1 V:pra0.1 P:pc0.2 P:pc1.1 P:pc1.2 P:pa0.3 V:s160.1 V:trq.1 V:totb0.1 V:l10.1 A:wb0.2 P:pa1.2
+V:cum1.1 P:pc0.3 V:sl0.1 V:c5.1 V:zq.1 V:pra1.1 P:pa1.3 V:mh1.1 V:l11.1 A:wb1.2 V:nc.1 V:totb1.1 P:pc1.3 V:cw0.1
+V:zd.1 V:prb0.1 V:sl1.1 V:se0.1 V:he0.1 A:rz00.1 P:pb0.1 P:pb1.1 P:pb0.2 V:sw.1 V:swb.1 V:l20.1 V:xsc00.1
+V:xsc00.2 V:low.1 A:rs.1 V:ywb0.1 A:tbb0.1 V:ywa0.1 A:tba0.1 V:cw1.1 swv00.1 V:ck00.1 sendup00.1 sendlow00.1
+G:wa.1 V:prb1.1 V:zw0.1 V:se1.1 V:he1.1 P:pb0.3 P:pb0.4 P:pb1.2 V:lao00.1 A:yl0.1 A:ylp0.1 A:su0.1 V:zw1.1
+V:l21.1 V:xsc10.1 V:xsc10.2 V:la00.1 pf00.1 pf00.2 senddown00.1 V:lb00.1 A:rz10.1 A:rs.2 V:ywb1.1 V:ywa1.1
+pm00.1 pm00.2 pn00.1 A:tbb1.1 swv10.1 A:tba1.1 V:ck10.1 sendup10.1 sendlow10.1 pq00.1 pn00.2 V:pl00.1 P:pd0.1
+V:pta0.1 V:ptb0.1 V:yo00_0.1 A:yl1.1 A:ga.1 P:pb1.3 P:pb1.4 A:su1.1 A:ylp1.1 V:lb10.1 V:la10.1 V:yo00_1.1
+P:pa0.4 V:lao10.1 V:hi0.2 V:hm0.2 V:ls01.1 V:mv0.1 V:totv0.1 pf10.1 pf10.2 senddown10.1 A:m10.2 P:pa0.5 V:cum0.2
+V:pra0.2 P:pa0.6 V:s160.2 pm10.1 V:l10.2 A:mh0.1 A:wc.1 pm10.2 pn10.1 pq10.1 P:pc0.4 V:wa.1 P:pb0.5 V:pl10.1
+pn10.2 P:pd1.1 V:pta1.1 V:ptb1.1 V:yo10_0.1 P:pc0.5 P:pc0.6 V:sl0.2 A:ga.2 V:yo10_1.1 V:cw0.2 P:pa1.4 V:hi1.2
+V:hm1.2 V:ls11.1 V:prb0.2 V:se0.2 V:he0.2 V:s161.2 A:m11.2 P:pa1.5 V:cum1.2 P:pb0.6 V:l20.2 V:pra1.2 P:pc1.4
+P:pc1.5 G:rz01.1 V:rz01.1 G:xw01.1 P:pa1.6 V:l11.2 G:xwa01.1 G:xwa11.1 G:xw11.1 V:xsc01.1 A:mh1.1 P:pc1.6
+V:sl1.2 V:xsc01.2 V:ywb0.2 V:ywa0.2 A:wb1.3 V:cw1.2 A:tbb0.2 swv01.1 P:pb0.7 A:tba0.2 V:ck01.1 V:prb1.2
+P:pb1.5 P:pb1.6 V:se1.2 V:he1.2 G:rz11.1 A:rz11.1 A:rs.3 V:lao01.1 V:l21.2 P:pb0.8 A:su0.2 V:xsc11.1 V:xsc11.2
+sendup01.1 sendlow01.1 V:la01.1 pf01.1 pf01.2 A:yl0.2 V:ywb1.2 A:tbb1.2 P:pb1.7 V:lb01.1 swv11.1 V:ywa1.2
+A:tba1.2 pm01.1 V:ck11.1 V:lao11.1 pm01.2 pn01.1 A:yl1.2 A:ylp0.2 senddown01.1 sendup11.1 sendlow11.1 V:la11.1
+pq01.1 pn01.2 pf11.1 pf11.2 V:pl01.1 P:pd0.2 V:ptb0.2 V:pta0.2 V:yo01_0.1 A:ga.3 A:ylp1.2 V:yo01_1.1 A:out011.1
+S:out000.1 S:out001.1 P:pb1.8 V:lb11.1 pm11.1 pm11.2 A:su1.2 A:out010.1 pn11.1 pq11.1 senddown11.1 V:pl11.1
+pn11.2 P:pd1.2 V:pta1.2 V:ptb1.2 V:yo11_0.1 S:out100.1 A:ga.4 V:yo11_1.1 A:out110.1 A:out111.1 S:out101.1 end.1
 """
 
 
@@ -174,16 +175,16 @@ def build(g, core, T, topo, rank):
     def wrap(bank, zz, src):
         return [(bank[:, 0:K], zz[:, 15 - i:143 - i], src[:, i:S:16]) for i in range(16)]
 
-    def send(pairs, width, sem, r, tag):
+    def send(pairs, first, sem, r, tag):
         transfers = []
         for n, (dst_rank, src, dst) in enumerate(pairs):
             c = T.cores[dst_rank]
             rid, pid = topo.addr(c)[0], topo.addr(c)[1]
-            eng = topo.engines(core, c)[n * width:(n + 1) * width]
+            eng = (topo.engines(core, c) * 2)[first + 2 * n:first + 2 * n + 2]
             transfers.append(RemoteDMATransfer(dst_ids=[DstId(rid=rid, pnc=pid)],
                                                dma_engine_mask=sum(1 << e for e in eng),
                                                remote_sem=T.sem[sem], src=src, dst=dst))
-        sent[0] += width * len(pairs)
+        sent[0] += 2 * len(pairs)
         rec("G", lambda: g.remote_dma_fused(transfers, local_sem=T.sem.sent), r, [], kind="remote", tag=tag)
 
     pf, af, g16, a4, c11, c5, cd, b256, low, ps = (T.col[:, j:j + 1] for j in range(10))
@@ -248,6 +249,8 @@ def build(g, core, T, topo, rank):
     for s in range(2):
         ts(T["zw%d" % s][:], T.z[:], T.ws[:, 4 * s:4 * s + 1], None, OP.mult, None,
            ["z", "ws%d0" % s, "ws%d1" % s], ["zw%d" % s])
+    fill(T.wc, 0, WP, 0, ["wc"])
+    fill(T.wa, 0, WP, 0, ["wa"])
     for n in ("10", "01", "11"):
         fill(T["xw" + n], 0, W, -256, ["xwa" + n])
         fill(T["xw" + n], W, 2 * W, -256, ["xw" + n])
@@ -266,28 +269,41 @@ def build(g, core, T, topo, rank):
         ts(b["hm"][:], b["hi"][:], M - 1, None, OP.bitwise_and, None, k("hi"), k("hm"))
         cp(ls[:], b["hm"][:], k("hm"), ["ls" + n])
         cp(b["s16"][:], b["hm"][:], k("hm"), k("s16"))
-        act(m1[:], T.tab1[:].indirect(ls[:]), ["tab1", "ls" + n], k("tota", "m1"), accum_out=tot[:, 0:1])
-        mm([(pa[:, 0:1], T.trs[:], tot[:, 0:1])], ["trs"] + k("tota"), k("pa"))
-        mm([(pc[:, 0:1], T.trs[:], tot[:, 0:1])], k("tota"), k("pc"))
-        mm([(pc[:, 1:2], T.tri[:], tot[:, 0:1])], ["tri"] + k("tota"), k("pc"))
+        cut = 640 if n == "01" else S
+        act(m1[:, 0:cut], T.tab1[:].indirect(ls[:, 0:cut // 16]), ["tab1", "ls" + n], k("tota", "m1"),
+            accum_out=tot[:, 0:1])
+        tots = [tot[:, 0:1]]
+        if cut < S:
+            cp(m1[:, cut:S], T.tab1[:].indirect(ls[:, cut // 16:K]), ["tab1", "ls" + n], k("mv"))
+            rec("V", lambda: V.tensor_reduce(tot[:, 1:2], m1[:, cut:S], AxisListType.X, OP.add), k("mv"), k("totv"))
+            tots.append(tot[:, 1:2])
+        mm([(pa[:, 0:1], T.trs[:], t) for t in tots], ["trs"] + k("tota", "totv"), k("pa"))
+        mm([(pc[:, 0:1], T.trs[:], t) for t in tots], ["trs"] + k("tota", "totv"), k("pc"))
+        mm([(pc[:, 1:2], T.tri[:], t) for t in tots], ["tri"] + k("tota", "totv"), k("pc"))
         if L == 0:
             ts(mh[:], T.tab2[:].indirect(ls[:]), 16.0, None, OP.mult, None, ["tab2", "ls" + n], k("mh"))
             rec("V", lambda: V.tensor_reduce(tot[:, 4:5], mh[:], AxisListType.X, OP.add), k("mh"), k("totb"))
         else:
             act(mh[:], T.tab2[:].indirect(ls[:]), ["tab2", "ls" + n], k("totb", "mh"), scale=16.0,
                 accum_out=tot[:, 4:5])
-        scan(b["cum"][:], m1[:], m1[:], pa[:, 0:1], OP.add, OP.max, k("m1"), k("pa", "cum"))
-        scan(b["pra"][:], b["cum"][:], m1[:], 0.0, OP.max, OP.mult, k("cum", "m1"), k("pra"))
+        scan(b["cum"][:], m1[:], m1[:], pa[:, 0:1], OP.add, OP.max, k("m1", "mv"), k("pa", "cum"))
+        scan(b["pra"][:], b["cum"][:], m1[:], 0.0, OP.max, OP.mult, k("cum", "m1", "mv"), k("pra"))
         mm(wrap(pa, T.z, b["pra"]), ["z"] + k("pra"), k("pa"))
         cp(b["l1"][:], pa[:, 0:K], [], k("pa", "l1"))
-        act(b["wb"][:, 0:S + 1].indirect(b["l1"][:]), mh[:], k("mh", "l1"), k("wb"), func=AF.Tanh)
+        if cut == S:
+            act(b["wb"][:, 0:S + 1].indirect(b["l1"][:]), mh[:], k("mh", "l1"), k("wb"), func=AF.Tanh)
+            d0, d1, op1, dk = b["wb"], b["wb"], OP.max, k("wb")
+        else:
+            act(T.wc[:, 0:S + 1].indirect(b["l1"][:, 0:cut // 16]), mh[:, 0:cut], k("mh", "l1"), ["wc"], func=AF.Tanh)
+            ts(T.wa[:, 0:S + 1].indirect(b["l1"][:, cut // 16:K]), mh[:, cut:S], 0.0625, 0.0, OP.mult, OP.add,
+               k("mh", "l1"), ["wa"])
+            d0, d1, op1, dk = T.wc, T.wa, OP.add, ["wc", "wa"]
         mm([(pc[:, 2:3], T.idf[:], c11), (pc[:, 2:3], T.trq[:], tot[:, 4:5])], ["idf", "c11", "trq"] + k("totb"),
            k("pc"))
-        mm([(pb[:, 0:K], T.i5[:], b["s16"][:])] + wrap(pb, T.zd, m1), ["i5", "zd"] + k("s16", "m1"), k("pb"),
+        mm([(pb[:, 0:K], T.i5[:], b["s16"][:])] + wrap(pb, T.zd, m1), ["i5", "zd"] + k("s16", "m1", "mv"), k("pb"),
            final=False)
         cp(b["sl"][:, 0:2], pc[:, 0:2], [], k("pc", "sl"))
-        scan(cw[:, 0:S + 1], b["wb"][:, 0:S + 1], b["wb"][:, 0:S + 1], pc[:, 2:3], OP.add, OP.max,
-             k("wb"), k("pc", "cw"))
+        scan(cw[:, 0:S + 1], d0[:, 0:S + 1], d1[:, 0:S + 1], pc[:, 2:3], OP.add, op1, dk, k("pc", "cw"))
         cwin = cw[:, 0:S + 1]
         tt(b["prb"][:], cwin.indirect(b["l1"][:]), mh[:], OP.mult, k("cw", "l1", "mh"), k("prb"))
         mm(wrap(pb, T.zq, b["prb"]), ["zq"] + k("prb"), k("pb"), first=False)
@@ -301,7 +317,8 @@ def build(g, core, T, topo, rank):
             act(rz[:].indirect(he[:, 0:16]), T.c16[:], ["c16"] + k("he"), ["rz" + n], func=AF.Tanh)
             act(T.rs[:], rz[:], ["rz" + n], ["rs"], scale=-1024.0, bias=512.0)
             cap, capk = T.rs, "rs"
-        src, srck = (b["xs"], ["xs%s0" % s, "xs%s1" % s]) if L == 0 else (T["yo%s0" % s], ["yo%s0_0" % s])
+        src, srck = (b["xs"], ["xs%s0" % s, "xs%s1" % s]) if L == 0 else \
+            (T["yo%s0" % s], ["yo%s0_0" % s, "yo%s0_1" % s])
         for j in range(2):
             cp(xw[:].indirect(b["l2"][:, 32 * j:32 * j + 32]), src[:, 512 * j:512 * j + 512], srck + k("l2"),
                ["xwa" + n, "xw" + n, "xsc" + n])
@@ -313,54 +330,62 @@ def build(g, core, T, topo, rank):
         if rank < NR - 1:
             mm([(pa[:, 0:H], T.sw[:], tb[:, H:M])], ["sw"] + k("tbb"), k("pa"), tag="swv" + n)
             tt(ck[:], tb[:, 0:H], pa[:, 0:H], OP.max, k("tba"), ["pa" + s, "ck" + n])
-            send([(o, ck[:, SL * o:SL * o + SL], la[:, SL * rank:SL * rank + SL]) for o in owners if o != rank], 2,
+        if rank in owners:
+            send([(o, ck[:, SL * o:SL * o + SL], la[:, SL * rank:SL * rank + SL]) for o in owners if o != rank], 0,
                  "up" + n, ["ck" + n], "sendup" + n)
-        if rank < NR // 2 - 1:
-            send([(r, ck[:], lb[:, H * rank:H * rank + H]) for r in range(rank + 1, NR // 2)], 2, "down" + n,
-                 ["ck" + n], "sendlow" + n)
+        mine = owners if rank in owners else upper
+        at = mine.index(rank)
+        if at < 3:
+            send([(r, ck[:], lb[:, H * at:H * at + H]) for r in reversed(mine[at + 1:])], 6 if rank in owners else 0,
+                 ("down" if rank in owners else "up") + n, ["ck" + n], "sendlow" + n)
         mm([(pb[:, 0:H], T.swb[:], tb[:, H:M])], ["swb"] + k("tbb"), k("pb"))
-        mm([(pb[:, H:M], T.swb[:], tb[:, 0:H])], k("tba"), k("pb"))
+        mm([(pb[:, H:M], T.swb[:], tb[:, 0:H])], ["swb"] + k("tba"), k("pb"))
         act(b["su"][:], pb[:], ["low"], k("pb", "su"), bias=low)
         act(b["yl"][:], yw[:].indirect(b["l2"][:]), k("ywa", "ywb", "l2"), k("yl"))
-        below, bk = pl[:], ["pl" + n]
+        act(pc[:], b["yl"][:, 512:S], k("yl"), k("pc", "ylp"))
         if rank in owners:
             own = slice(SL * rank, SL * rank + SL)
             cp(la[:, own], ck[:, own], ["ck" + n], ["lao" + n])
-            rec("V", None, [], ["la" + n], kind="arrival", sem="up" + n, val=2 * (NR - 2))
+            rec("V", None, [], ["la" + n], kind="arrival", sem="up" + n, val=6)
             tt(pfx[:, 0:2 * SL], la[:, 0:2 * SL], la[:, 2 * SL:4 * SL], OP.max, ["la" + n, "lao" + n], ["pfp" + n],
                tag="pf" + n)
-            x0, x1, key = pfx[:, 0:SL], pfx[:, SL:2 * SL], "pfp" + n
-            for r in upper:
-                tt(pfx[:, SL * r:SL * r + SL], x0, x1, OP.max, [key], ["pf%s_%d" % (n, r)], tag="pf" + n)
-                x0, x1, key = pfx[:, SL * r:SL * r + SL], la[:, SL * r:SL * r + SL], "pf%s_%d" % (n, r)
-            send([(r, pfx[:, SL * r:SL * r + SL], pl[:, own]) for r in upper], 2, "down" + n,
-                 ["pf%s_%d" % (n, r) for r in upper], "senddown" + n)
-            if rank > 0:
-                rec("V", None, [], ["lb" + n], kind="arrival", sem="down" + n, val=2 * rank)
-                below, bk = lb[:, 0:H], ["lb" + n]
-                for r in range(1, rank):
-                    tt(pl[:], below, lb[:, H * r:H * r + H], OP.max, bk + ["lb" + n], ["pl" + n], tag="pm" + n)
-                    below, bk = pl[:], ["pl" + n]
-        else:
-            rec("V", None, [], ["pl" + n], kind="arrival", sem="down" + n, val=2 * len(owners))
+            tt(pfx[:, H:H + SL], pfx[:, 0:SL], pfx[:, SL:2 * SL], OP.max, ["pfp" + n], ["pfm" + n], tag="pf" + n)
+            send([(r, pfx[:, H:H + SL], pl[:, own]) for r in upper], 0, "down" + n, ["pfm" + n], "senddown" + n)
+        near = pl[:] if rank in owners else pfx[:, 0:H]
+        below, bk = lb[:, 0:H], ["lb" + n]
+        if at > 0:
+            rec("V", None, [], ["lb" + n], kind="arrival", sem=("down" if rank in owners else "up") + n, val=2 * at)
+            for r in range(1, at):
+                tt(near, below, lb[:, H * r:H * r + H], OP.max, bk + ["lb" + n], ["near" + n], tag="pm" + n)
+                below, bk = near, ["near" + n]
+        if rank in upper:
+            rec("V", None, [], ["pl" + n], kind="arrival", sem="down" + n, val=8)
+            if at > 0:
+                mm([(pd[:, 0:H], T.sw[:], below)], ["sw"] + bk, k("pd"), tag="pq" + n)
+                tt(b["su"][:, 0:H], below, b["su"][:, 0:H], OP.max, bk, k("su"), tag="pn" + n)
+                tt(b["su"][:, H:M], b["su"][:, H:M], pd[:, 0:H], OP.max, [], k("pd", "su"), tag="pn" + n)
+            below, bk = pl[:], ["pl" + n]
         table, tk = b["su"], k("su")
         if rank > 0:
             mm([(pd[:, 0:H], T.sw[:], below)], ["sw"] + bk, k("pd"))
             tt(b["pt"][:, 0:H], below, b["su"][:, 0:H], OP.max, bk + k("su"), k("pta"))
             tt(b["pt"][:, H:M], b["su"][:, H:M], pd[:, 0:H], OP.max, k("su"), k("pd", "ptb"))
             table, tk = b["pt"], k("pta", "ptb")
-        cuts = [0, S] if L == 0 else [0, 640, S]
-        for j in range(len(cuts) - 1):
-            lo, hi = cuts[j], cuts[j + 1]
+        act(T.ga[:], table[:].indirect(ls[:, 32:K]), tk + ["ls" + n], ["ga"])
+        for j in range(2):
+            lo, hi = 512 * j, 512 * j + 512
             key = "yo%s_%d" % (n, j)
-            tt(yo[:, lo:hi], table[:].indirect(ls[:, lo // 16:hi // 16]), b["yl"][:, lo:hi], OP.max,
-               tk + ["ls" + n] + k("yl"), [key])
+            if j == 0:
+                tt(yo[:, lo:hi], table[:].indirect(ls[:, 0:32]), b["yl"][:, lo:hi], OP.max,
+                   tk + ["ls" + n] + k("yl"), [key])
+            else:
+                tt(yo[:, lo:hi], T.ga[:], pc[:], OP.max, ["ga"] + k("ylp"), ["pc" + s, key])
             if L == 1:
                 for h in range(2):
                     dma("SA"[h], T.y[64 * st:64 * st + 64, S * h + lo:S * h + hi], yo[64 * h:64 * h + 64, lo:hi],
                         [key], ["out%d%d%d" % (st, h, j)], "st%d%d%d" % (st, h, j))
         if L == 0:
-            mm(wrap(pa, b["zw"], yo), ["yo%s_0" % n] + k("zw"), k("pa"))
+            mm(wrap(pa, b["zw"], yo), ["yo%s_0" % n, "yo%s_1" % n] + k("zw"), k("pa"))
 
     for L in range(2):
         for st in range(2):

from concourse.bass import DstId, RemoteDMATransfer
from concourse.mybir import AluOpType, ActivationFunctionType, AxisListType

S = 1024
M = 512
H = M // 2
NR = 8
SL = 64
W = S + H
WP = 1040
K = S // 16

F32, BF, F16, I32, U16 = "float32", "bfloat16", "float16", "int32", "uint16"
SCRATCH = {"ci": ("sbuf", [128, 8, 16], I32), "cf": ("sbuf", [128, 8, 16], F16), "ex": ("sbuf", [128, 8, 128], F16)}
for _name, _cols, _dt in (
        ("pci", 8, I32), ("ai", 8, I32), ("col", 16, F32), ("ws", 8, F32), ("cc", 144, F32), ("t1", M, BF),
        ("t2", M, BF), ("tab1", M, BF), ("tab2", M, BF), ("gm", 8, F32), ("z", 144, BF), ("zq", 144, BF),
        ("zd", 144, F16), ("z2", 80, BF), ("bk", 128, F32), ("trs", 128, F32), ("tri", 128, F32), ("trq", 128, F32),
        ("idf", 128, F32), ("i5", 128, BF), ("sw", 128, BF), ("swb", 128, BF), ("i32", 32, F32), ("nc", 32, F32),
        ("lows", H, BF), ("c16", H, F32), ("rs", W, BF), ("ga", 512, BF), ("wc", WP, F32), ("wa", WP, F32)):
    SCRATCH[_name] = ("sbuf", [128, _cols], _dt)
STREAM = (("xs", S, BF), ("yl", S, BF), ("zw", 144, BF), ("hi", K, I32), ("hm", K, I32), ("s16", K, F16), ("l1", K, U16),
          ("l2", K, U16), ("sl", 16, U16), ("se", 32, F32), ("he", 32, U16), ("tot", 8, F32), ("m1", S, BF),
          ("cum", S, F16), ("pra", S, F16), ("prb", S, F16), ("mh", S, F32), ("wb", WP, F32), ("cw", WP, F32),
          ("yw", 2 * W, BF), ("tb", M, BF), ("su", M, BF), ("pt", M, BF))
for _s in "01":
    for _name, _cols, _dt in STREAM:
        SCRATCH[_name + _s] = ("sbuf", [128, _cols], _dt)
    for _name in ("pa", "pb", "pc", "pd"):
        SCRATCH[_name + _s] = ("psum", [128, 512], F32)
    for _l in "01":
        for _name, _cols, _dt in (("yo", S, BF), ("ls", K, U16), ("xw", 2 * W, BF), ("ck", H, BF), ("la", NR * SL, BF),
                                  ("rz", W, BF if _s + _l == "01" else F32), ("lb", 3 * H, BF), ("pf", NR * SL, BF),
                                  ("pl", H, BF)):
            SCRATCH[_name + _s + _l] = ("sbuf", [128, _cols], _dt)
SEMAPHORES = ["cV", "cA", "cP", "cG", "sent"] + \
    [a + s + h for a in ("dslot", "dx", "dw", "up", "down") for s in "01" for h in "01"] + \
    ["st" + s + h + j for s in "01" for h in "01" for j in "01"]

OP = AluOpType
AF = ActivationFunctionType

ORDER = """
S:ci00.1 S:ci10.1 A:ci01.1 A:ci11.1 S:xs00.1 S:xs01.1 S:xs10.1 S:xs11.1 S:ws00.1 S:ws01.1 S:ws10.1 S:ws11.1
V:xw00.1 G:pci.1 V:pf.1 G:cc.1 A:wb0.1 A:wb1.1 V:ai.1 V:idf.1 V:af.1 V:b256.1 V:g16.1 V:i5.1 V:ps.1 V:bk.1 V:gm.1
V:a4.1 V:z.1 V:z2.1 V:cf.1 V:ex3.1 V:ex2.1 V:ex7.1 V:ex5.1 V:ex0.1 V:ex4.1 V:ex6.1 V:ex1.1 G:t1.1 G:t2.1 V:c11.1
V:tab1.1 P:pa0.1 V:hi0.1 P:pa1.1 V:hi1.1 V:hm0.1 V:hm1.1 V:ls00.1 A:m10.1 V:tab2.1 V:ls10.1 A:m11.1 V:s161.1
V:mh0.1 G:trs.1 G:i32.1 G:tri.1 G:c16.1 G:rz00.1 G:xwa10.1 G:rz10.1 G:xw10.1 G:wc.1 G:lows.1 P:pa0.2 P:pc0.1
V:cum0.1 V:cd.1 V:pra0.1 P:pc0.2 P:pc1.1 P:pc1.2 P:pa0.3 V:s160.1 V:trq.1 V:totb0.1 V:l10.1 A:wb0.2 P:pa1.2
V:cum1.1 P:pc0.3 V:sl0.1 V:c5.1 V:zq.1 V:pra1.1 P:pa1.3 V:mh1.1 V:l11.1 A:wb1.2 V:nc.1 V:totb1.1 P:pc1.3 V:cw0.1
V:zd.1 V:prb0.1 V:sl1.1 V:se0.1 V:he0.1 A:rz00.1 P:pb0.1 P:pb1.1 P:pb0.2 V:sw.1 V:swb.1 V:l20.1 V:xsc00.1
V:xsc00.2 V:low.1 A:rs.1 V:ywb0.1 A:tbb0.1 V:ywa0.1 A:tba0.1 V:cw1.1 swv00.1 V:ck00.1 sendup00.1 sendlow00.1
G:wa.1 V:prb1.1 V:zw0.1 V:se1.1 V:he1.1 P:pb0.3 P:pb0.4 P:pb1.2 V:lao00.1 A:yl0.1 A:ylp0.1 A:su0.1 V:zw1.1
V:l21.1 V:xsc10.1 V:xsc10.2 V:la00.1 pf00.1 pf00.2 senddown00.1 V:lb00.1 A:rz10.1 A:rs.2 V:ywb1.1 V:ywa1.1
pm00.1 pm00.2 pn00.1 A:tbb1.1 swv10.1 A:tba1.1 V:ck10.1 sendup10.1 sendlow10.1 pq00.1 pn00.2 V:pl00.1 P:pd0.1
V:pta0.1 V:ptb0.1 V:yo00_0.1 A:yl1.1 A:ga.1 P:pb1.3 P:pb1.4 A:su1.1 A:ylp1.1 V:lb10.1 V:la10.1 V:yo00_1.1
P:pa0.4 V:lao10.1 V:hi0.2 V:hm0.2 V:ls01.1 V:mv0.1 V:totv0.1 pf10.1 pf10.2 senddown10.1 A:m10.2 P:pa0.5 V:cum0.2
V:pra0.2 P:pa0.6 V:s160.2 pm10.1 V:l10.2 A:mh0.1 A:wc.1 pm10.2 pn10.1 pq10.1 P:pc0.4 V:wa.1 P:pb0.5 V:pl10.1
pn10.2 P:pd1.1 V:pta1.1 V:ptb1.1 V:yo10_0.1 P:pc0.5 P:pc0.6 V:sl0.2 A:ga.2 V:yo10_1.1 V:cw0.2 P:pa1.4 V:hi1.2
V:hm1.2 V:ls11.1 V:prb0.2 V:se0.2 V:he0.2 V:s161.2 A:m11.2 P:pa1.5 V:cum1.2 P:pb0.6 V:l20.2 V:pra1.2 P:pc1.4
P:pc1.5 G:rz01.1 V:rz01.1 G:xw01.1 P:pa1.6 V:l11.2 G:xwa01.1 G:xwa11.1 G:xw11.1 V:xsc01.1 A:mh1.1 P:pc1.6
V:sl1.2 V:xsc01.2 V:ywb0.2 V:ywa0.2 A:wb1.3 V:cw1.2 A:tbb0.2 swv01.1 P:pb0.7 A:tba0.2 V:ck01.1 V:prb1.2
P:pb1.5 P:pb1.6 V:se1.2 V:he1.2 G:rz11.1 A:rz11.1 A:rs.3 V:lao01.1 V:l21.2 P:pb0.8 A:su0.2 V:xsc11.1 V:xsc11.2
sendup01.1 sendlow01.1 V:la01.1 pf01.1 pf01.2 A:yl0.2 V:ywb1.2 A:tbb1.2 P:pb1.7 V:lb01.1 swv11.1 V:ywa1.2
A:tba1.2 pm01.1 V:ck11.1 V:lao11.1 pm01.2 pn01.1 A:yl1.2 A:ylp0.2 senddown01.1 sendup11.1 sendlow11.1 V:la11.1
pq01.1 pn01.2 pf11.1 pf11.2 V:pl01.1 P:pd0.2 V:ptb0.2 V:pta0.2 V:yo01_0.1 A:ga.3 A:ylp1.2 V:yo01_1.1 A:out011.1
S:out000.1 S:out001.1 P:pb1.8 V:lb11.1 pm11.1 pm11.2 A:su1.2 A:out010.1 pn11.1 pq11.1 senddown11.1 V:pl11.1
pn11.2 P:pd1.2 V:pta1.2 V:ptb1.2 V:yo11_0.1 S:out100.1 A:ga.4 V:yo11_1.1 A:out110.1 A:out111.1 S:out101.1 end.1
"""


def needs(ops):
    writer, readers, res = {}, {}, []
    for n, o in enumerate(ops):
        deps = set()
        for k in o["r"] + o["w"]:
            if k in writer:
                deps.add(writer[k])
        for k in o["w"]:
            deps.update(readers.get(k, []))
        res.append(deps)
        if o["kind"] != "remote":
            for k in o["r"]:
                readers.setdefault(k, []).append(n)
        for k in o["w"]:
            writer[k] = n
            readers[k] = []
    return res


def emit(g, T, ops):
    queue = {"V": g.vector, "A": g.scalar, "P": g.tensor, "G": g, "S": g.sync}
    waited, need = {}, []
    for o, deps in zip(ops, needs(ops)):
        last = {}
        for d in deps:
            p = ops[d]
            if p["e"] == "P" and o["e"] == "P" and p["sem"] is None:
                continue
            key = p["sem"] if p["sem"] is not None else p["e"]
            last[key] = max(last.get(key, -1), d)
        mine = []
        for key in sorted(last):
            d = last[key]
            if waited.get((o["e"], key), -1) < d:
                waited[(o["e"], key)] = d
                ops[d]["sig"] = True
                mine.append(d)
        need.append(mine)
    count = {"V": 0, "A": 0, "P": 0, "G": 0}
    for o, mine in zip(ops, need):
        for d in mine:
            p = ops[d]
            queue[o["e"]].wait_ge(T.sem[p["sem"] if p["sem"] is not None else "c" + p["e"]], p["val"])
        if o["fn"] is None:
            continue
        ins = o["fn"]()
        if o["kind"] == "dma":
            ins.then_inc(T.sem[o["sem"]], 16)
        elif o["kind"] == "compute" and o["sig"]:
            count[o["e"]] += 1
            o["val"] = count[o["e"]]
            ins.then_inc(T.sem["c" + o["e"]], 1)


def build(g, core, T, topo, rank):
    ops, sent, seen = [], [0], {}
    V, A, P = g.vector, g.scalar, g.tensor

    def rec(e, fn, r, w, kind="compute", sem=None, val=0, tag=None):
        tag = tag if tag is not None else e + ":" + w[-1]
        seen[tag] = seen.get(tag, 0) + 1
        ops.append({"e": e, "fn": fn, "r": list(r), "w": list(w), "kind": kind, "sem": sem, "val": val,
                    "sig": False, "tag": tag + "." + str(seen[tag])})

    def dma(e, out, in_, r, w, sem):
        q = g.sync if e == "S" else A
        rec(e, lambda: q.dma_start(out, in_), r, w, kind="dma", sem=sem, val=16)

    def ts(out, in0, s1, s2, op0, op1, r, w):
        if op1 is None:
            rec("V", lambda: V.tensor_scalar(out, in0, s1, None, op0), r, w)
        else:
            rec("V", lambda: V.tensor_scalar(out, in0, s1, s2, op0, op1), r, w)

    def cp(out, in_, r, w):
        rec("V", lambda: V.tensor_copy(out, in_), r, w)

    def tt(out, a, b, op, r, w, tag=None):
        rec("V", lambda: V.tensor_tensor(out, a, b, op), r, w, tag=tag)

    def scan(out, d0, d1, init, op0, op1, r, w):
        rec("V", lambda: V.tensor_tensor_scan(out, d0, d1, init, op0, op1), r, w)

    def act(out, in_, r, w, func=AF.Identity, **kw):
        rec("A", lambda: A.activation(out, in_, func, **kw), r, w)

    def iota(out, pattern, base, mult, w, whole=False):
        if whole:
            rec("G", lambda: g.iota(out, pattern, base, mult), [], w)
        else:
            rec("G", lambda: g.iota(out, pattern, base, mult, allow_small_or_imprecise_dtypes=True), [], w)

    def fill(buf, lo, hi, value, w):
        iota(buf[:, lo:hi], [[0, hi - lo]], value, 0, w)

    def mm(items, r, w, first=True, final=True, tag=None):
        def fn():
            ins = None
            for n, (out, lhsT, rhs) in enumerate(items):
                ins = P.matmul(out, lhsT, rhs, first and n == 0, final and n == len(items) - 1)
            return ins
        rec("P", fn, r, w, tag=tag)

    def wrap(bank, zz, src):
        return [(bank[:, 0:K], zz[:, 15 - i:143 - i], src[:, i:S:16]) for i in range(16)]

    def send(pairs, first, sem, r, tag):
        transfers = []
        for n, (dst_rank, src, dst) in enumerate(pairs):
            c = T.cores[dst_rank]
            rid, pid = topo.addr(c)[0], topo.addr(c)[1]
            eng = (topo.engines(core, c) * 2)[first + 2 * n:first + 2 * n + 2]
            transfers.append(RemoteDMATransfer(dst_ids=[DstId(rid=rid, pnc=pid)],
                                               dma_engine_mask=sum(1 << e for e in eng),
                                               remote_sem=T.sem[sem], src=src, dst=dst))
        sent[0] += 2 * len(pairs)
        rec("G", lambda: g.remote_dma_fused(transfers, local_sem=T.sem.sent), r, [], kind="remote", tag=tag)

    pf, af, g16, a4, c11, c5, cd, b256, low, ps = (T.col[:, j:j + 1] for j in range(10))

    cik = ["ci00", "ci01", "ci10", "ci11"]
    for s in range(2):
        for h in range(2):
            dma("SA"[h], T.ci[64 * h:64 * h + 64, 4 * s:4 * s + 4, :], T.slot[4 * s:4 * s + 4, S * h:S * h + S],
                [], ["ci%d%d" % (s, h)], "dslot%d%d" % (s, h))
    for s in range(2):
        for h in range(2):
            dma("S", T["xs%d" % s][64 * h:64 * h + 64, :], T.x[64 * s:64 * s + 64, S * h:S * h + S],
                cik, ["xs%d%d" % (s, h)], "dx%d%d" % (s, h))
    for s in range(2):
        for h in range(2):
            dma("S", T.ws[64 * h:64 * h + 64, 4 * s:4 * s + 1], T.w[64 * s:64 * s + 64, :],
                [], ["ws%d%d" % (s, h)], "dw%d%d" % (s, h))
    rec("V", lambda: V.memset(T.xw00[:], -256.0), [], ["xwa00", "xw00"])
    iota(T.pci[:, 0:1], [[0, 1]], 0, 1, ["pci"], whole=True)
    iota(T.cc[:], [[1, 144]], 0, 0, ["cc"])
    iota(T.t1[:], [[0, 2], [1, 16], [0, 16]], 0, 0, ["t1"])
    for s in "01":
        act(T["wb" + s][:, 0:16], T.cc[:, 0:16], ["cc"], ["wb" + s], func=AF.Tanh, scale=0.0)
    ts(T.ai[:, 0:1], T.pci[:, 0:1], 15, None, OP.bitwise_and, None, ["pci"], ["ai"])
    cp(pf, T.pci[:, 0:1], ["pci"], ["pf"])
    cp(af, T.ai[:, 0:1], ["ai"], ["af"])
    ts(g16, pf, af, None, OP.subtract, None, ["pf", "af"], ["g16"])
    ts(a4, af, 4.0, None, OP.mult, None, ["af"], ["a4"])
    ts(b256, pf, 64.0, 256.0, OP.is_ge, OP.mult, ["pf"], ["b256"])
    ts(T.bk[:], T.cc[:, 0:128], g16, 15.0, OP.subtract, OP.is_le, ["cc", "g16"], ["bk"])
    ts(T.gm[:], T.cc[:, 0:128:16], g16, None, OP.is_equal, None, ["cc", "g16"], ["gm"])
    ts(T.z2[:], T.cc[:, 0:80], a4, 3.0, OP.subtract, OP.is_equal, ["cc", "a4"], ["z2"])
    ts(T.z[:], T.cc[:], g16, 15.0, OP.subtract, OP.is_equal, ["cc", "g16"], ["z"])
    ts(T.tab1[:], T.t1[:], af, None, OP.is_equal, None, ["t1", "af"], ["tab1"])
    rec("G", lambda: g.affine_select(T.trs[:], T.bk[:], [[1, 128]], OP.is_gt, 0.0, 0, -1), ["bk"], ["trs"])
    iota(T.t2[:], [[0, 32], [1, 16]], 0, 0, ["t2"])
    rec("G", lambda: g.affine_select(T.tri[:], T.bk[:], [[1, 128]], OP.is_ge, 0.0, 0, -1), ["bk"], ["tri"])
    iota(T.i32[:], [[0, 2], [1, 16]], 0, 0, ["i32"])
    fill(T.lows, 0, H, -256, ["lows"])
    fill(T.c16, 0, H, 16, ["c16"])
    fill(T.rz00, 0, W, 0, ["rz00"])
    cp(T.cf[:], T.ci[:], cik, ["cf"])
    for h in range(8):
        ts(T.ex[:, :, 16 * h:16 * h + 16], T.cf[:], T.gm[:, h:h + 1], None, OP.mult, None, ["cf", "gm"], ["ex%d" % h])
    for s in range(2):
        mm([(T["pa%d" % s][:, 0:K], T.ex[:, 4 * s + b, :], T.z2[:, 3 - b:3 - b + K]) for b in range(4)],
           ["ex%d" % h for h in range(8)] + ["z2"], ["pa%d" % s])
    ts(T.tab2[:], T.t2[:], af, None, OP.is_equal, None, ["t2", "af"], ["tab2"])
    ts(cd, af, -79.0, None, OP.mult, None, ["af"], ["cd"])
    ts(c11, af, 11.0, None, OP.mult, None, ["af"], ["c11"])
    ts(c5, af, 5.0, 0.25, OP.mult, OP.add, ["af"], ["c5"])
    ts(low, b256, -256.0, None, OP.add, None, ["b256"], ["low"])
    ts(ps, b256, -0.5, pf, OP.mult, OP.add, ["b256", "pf"], ["ps"])
    ts(T.zd[:], T.z[:], cd, None, OP.mult, None, ["z", "cd"], ["zd"])
    ts(T.i5[:], T.cc[:, 0:128], pf, 5.0, OP.is_equal, OP.mult, ["cc", "pf"], ["i5"])
    ts(T.idf[:], T.cc[:, 0:128], pf, None, OP.is_equal, None, ["cc", "pf"], ["idf"])
    ts(T.trq[:], T.trs[:], 0.0625, None, OP.mult, None, ["trs"], ["trq"])
    ts(T.zq[:], T.z[:], 0.0625, None, OP.mult, None, ["z"], ["zq"])
    ts(T.nc[:], T.i32[:], c5, None, OP.add, None, ["i32", "c5"], ["nc"])
    ts(T.sw[:], T.cc[:, 0:128], ps, 64.0, OP.subtract, OP.is_equal, ["cc", "ps"], ["sw"])
    ts(T.swb[:], T.cc[:, 0:128], pf, 64.0, OP.subtract, OP.is_equal, ["cc", "pf"], ["swb"])
    for s in range(2):
        ts(T["zw%d" % s][:], T.z[:], T.ws[:, 4 * s:4 * s + 1], None, OP.mult, None,
           ["z", "ws%d0" % s, "ws%d1" % s], ["zw%d" % s])
    fill(T.wc, 0, WP, 0, ["wc"])
    fill(T.wa, 0, WP, 0, ["wa"])
    for n in ("10", "01", "11"):
        fill(T["xw" + n], 0, W, -256, ["xwa" + n])
        fill(T["xw" + n], W, 2 * W, -256, ["xw" + n])
        fill(T["rz" + n], 0, W, 256 if n == "01" else 0, ["rz" + n])

    def layer(st, L):
        s, n = str(st), "%d%d" % (st, L)
        b = {x[0]: T[x[0] + s] for x in STREAM}
        ls, xw, rz, ck, la, lb, pfx, pl, yo = (T[x + n] for x in ("ls", "xw", "rz", "ck", "la", "lb", "pf", "pl", "yo"))
        pa, pb, pc, pd, tot, m1, mh, cw, yw, tb, he = (T[x + s] for x in ("pa", "pb", "pc", "pd", "tot", "m1", "mh",
                                                                          "cw", "yw", "tb", "he"))

        def k(*names):
            return [x + s for x in names]
        ts(b["hi"][:], pa[:, 0:K], b256, None, OP.add, None, ["b256"], k("pa", "hi"))
        ts(b["hm"][:], b["hi"][:], M - 1, None, OP.bitwise_and, None, k("hi"), k("hm"))
        cp(ls[:], b["hm"][:], k("hm"), ["ls" + n])
        cp(b["s16"][:], b["hm"][:], k("hm"), k("s16"))
        cut = 640 if n == "01" else S
        act(m1[:, 0:cut], T.tab1[:].indirect(ls[:, 0:cut // 16]), ["tab1", "ls" + n], k("tota", "m1"),
            accum_out=tot[:, 0:1])
        tots = [tot[:, 0:1]]
        if cut < S:
            cp(m1[:, cut:S], T.tab1[:].indirect(ls[:, cut // 16:K]), ["tab1", "ls" + n], k("mv"))
            rec("V", lambda: V.tensor_reduce(tot[:, 1:2], m1[:, cut:S], AxisListType.X, OP.add), k("mv"), k("totv"))
            tots.append(tot[:, 1:2])
        mm([(pa[:, 0:1], T.trs[:], t) for t in tots], ["trs"] + k("tota", "totv"), k("pa"))
        mm([(pc[:, 0:1], T.trs[:], t) for t in tots], ["trs"] + k("tota", "totv"), k("pc"))
        mm([(pc[:, 1:2], T.tri[:], t) for t in tots], ["tri"] + k("tota", "totv"), k("pc"))
        if L == 0:
            ts(mh[:], T.tab2[:].indirect(ls[:]), 16.0, None, OP.mult, None, ["tab2", "ls" + n], k("mh"))
            rec("V", lambda: V.tensor_reduce(tot[:, 4:5], mh[:], AxisListType.X, OP.add), k("mh"), k("totb"))
        else:
            act(mh[:], T.tab2[:].indirect(ls[:]), ["tab2", "ls" + n], k("totb", "mh"), scale=16.0,
                accum_out=tot[:, 4:5])
        scan(b["cum"][:], m1[:], m1[:], pa[:, 0:1], OP.add, OP.max, k("m1", "mv"), k("pa", "cum"))
        scan(b["pra"][:], b["cum"][:], m1[:], 0.0, OP.max, OP.mult, k("cum", "m1", "mv"), k("pra"))
        mm(wrap(pa, T.z, b["pra"]), ["z"] + k("pra"), k("pa"))
        cp(b["l1"][:], pa[:, 0:K], [], k("pa", "l1"))
        if cut == S:
            act(b["wb"][:, 0:S + 1].indirect(b["l1"][:]), mh[:], k("mh", "l1"), k("wb"), func=AF.Tanh)
            d0, d1, op1, dk = b["wb"], b["wb"], OP.max, k("wb")
        else:
            act(T.wc[:, 0:S + 1].indirect(b["l1"][:, 0:cut // 16]), mh[:, 0:cut], k("mh", "l1"), ["wc"], func=AF.Tanh)
            ts(T.wa[:, 0:S + 1].indirect(b["l1"][:, cut // 16:K]), mh[:, cut:S], 0.0625, 0.0, OP.mult, OP.add,
               k("mh", "l1"), ["wa"])
            d0, d1, op1, dk = T.wc, T.wa, OP.add, ["wc", "wa"]
        mm([(pc[:, 2:3], T.idf[:], c11), (pc[:, 2:3], T.trq[:], tot[:, 4:5])], ["idf", "c11", "trq"] + k("totb"),
           k("pc"))
        mm([(pb[:, 0:K], T.i5[:], b["s16"][:])] + wrap(pb, T.zd, m1), ["i5", "zd"] + k("s16", "m1", "mv"), k("pb"),
           final=False)
        cp(b["sl"][:, 0:2], pc[:, 0:2], [], k("pc", "sl"))
        scan(cw[:, 0:S + 1], d0[:, 0:S + 1], d1[:, 0:S + 1], pc[:, 2:3], OP.add, op1, dk, k("pc", "cw"))
        cwin = cw[:, 0:S + 1]
        tt(b["prb"][:], cwin.indirect(b["l1"][:]), mh[:], OP.mult, k("cw", "l1", "mh"), k("prb"))
        mm(wrap(pb, T.zq, b["prb"]), ["zq"] + k("prb"), k("pb"), first=False)
        tt(b["se"][:], cwin.indirect(b["sl"][:, 0:2]), T.nc[:], OP.add, ["nc"] + k("cw", "sl"), k("se"))
        cp(he[:], b["se"][:], k("se"), k("he"))
        ts(b["l2"][:], pb[:, 0:K], 0.25, None, OP.add, None, [], k("pb", "l2"))
        if n == "01":
            cp(rz[:].indirect(he[:, 0:16]), T.lows[:], ["lows"] + k("he"), ["rz" + n])
            cap, capk = rz, "rz" + n
        else:
            act(rz[:].indirect(he[:, 0:16]), T.c16[:], ["c16"] + k("he"), ["rz" + n], func=AF.Tanh)
            act(T.rs[:], rz[:], ["rz" + n], ["rs"], scale=-1024.0, bias=512.0)
            cap, capk = T.rs, "rs"
        src, srck = (b["xs"], ["xs%s0" % s, "xs%s1" % s]) if L == 0 else \
            (T["yo%s0" % s], ["yo%s0_0" % s, "yo%s0_1" % s])
        for j in range(2):
            cp(xw[:].indirect(b["l2"][:, 32 * j:32 * j + 32]), src[:, 512 * j:512 * j + 512], srck + k("l2"),
               ["xwa" + n, "xw" + n, "xsc" + n])
        scan(yw[:, W:2 * W], cap[:], xw[:, W:2 * W], -256.0, OP.min, OP.max, ["xw" + n, capk], k("ywb"))
        scan(yw[:, 0:W], cap[:], xw[:, 0:W], -256.0, OP.min, OP.max, ["xw" + n, capk], k("ywa"))
        act(tb[:, H:M], yw[:, W:2 * W].indirect(he[:, 16:32]), k("ywb", "he"), k("tbb"))
        act(tb[:, 0:H], yw[:, 0:W].indirect(he[:, 16:32]), k("ywa", "he"), k("tba"))
        owners, upper = list(range(NR // 2)), list(range(NR // 2, NR))
        if rank < NR - 1:
            mm([(pa[:, 0:H], T.sw[:], tb[:, H:M])], ["sw"] + k("tbb"), k("pa"), tag="swv" + n)
            tt(ck[:], tb[:, 0:H], pa[:, 0:H], OP.max, k("tba"), ["pa" + s, "ck" + n])
        if rank in owners:
            send([(o, ck[:, SL * o:SL * o + SL], la[:, SL * rank:SL * rank + SL]) for o in owners if o != rank], 0,
                 "up" + n, ["ck" + n], "sendup" + n)
        mine = owners if rank in owners else upper
        at = mine.index(rank)
        if at < 3:
            send([(r, ck[:], lb[:, H * at:H * at + H]) for r in reversed(mine[at + 1:])], 6 if rank in owners else 0,
                 ("down" if rank in owners else "up") + n, ["ck" + n], "sendlow" + n)
        mm([(pb[:, 0:H], T.swb[:], tb[:, H:M])], ["swb"] + k("tbb"), k("pb"))
        mm([(pb[:, H:M], T.swb[:], tb[:, 0:H])], ["swb"] + k("tba"), k("pb"))
        act(b["su"][:], pb[:], ["low"], k("pb", "su"), bias=low)
        act(b["yl"][:], yw[:].indirect(b["l2"][:]), k("ywa", "ywb", "l2"), k("yl"))
        act(pc[:], b["yl"][:, 512:S], k("yl"), k("pc", "ylp"))
        if rank in owners:
            own = slice(SL * rank, SL * rank + SL)
            cp(la[:, own], ck[:, own], ["ck" + n], ["lao" + n])
            rec("V", None, [], ["la" + n], kind="arrival", sem="up" + n, val=6)
            tt(pfx[:, 0:2 * SL], la[:, 0:2 * SL], la[:, 2 * SL:4 * SL], OP.max, ["la" + n, "lao" + n], ["pfp" + n],
               tag="pf" + n)
            tt(pfx[:, H:H + SL], pfx[:, 0:SL], pfx[:, SL:2 * SL], OP.max, ["pfp" + n], ["pfm" + n], tag="pf" + n)
            send([(r, pfx[:, H:H + SL], pl[:, own]) for r in upper], 0, "down" + n, ["pfm" + n], "senddown" + n)
        near = pl[:] if rank in owners else pfx[:, 0:H]
        below, bk = lb[:, 0:H], ["lb" + n]
        if at > 0:
            rec("V", None, [], ["lb" + n], kind="arrival", sem=("down" if rank in owners else "up") + n, val=2 * at)
            for r in range(1, at):
                tt(near, below, lb[:, H * r:H * r + H], OP.max, bk + ["lb" + n], ["near" + n], tag="pm" + n)
                below, bk = near, ["near" + n]
        if rank in upper:
            rec("V", None, [], ["pl" + n], kind="arrival", sem="down" + n, val=8)
            if at > 0:
                mm([(pd[:, 0:H], T.sw[:], below)], ["sw"] + bk, k("pd"), tag="pq" + n)
                tt(b["su"][:, 0:H], below, b["su"][:, 0:H], OP.max, bk, k("su"), tag="pn" + n)
                tt(b["su"][:, H:M], b["su"][:, H:M], pd[:, 0:H], OP.max, [], k("pd", "su"), tag="pn" + n)
            below, bk = pl[:], ["pl" + n]
        table, tk = b["su"], k("su")
        if rank > 0:
            mm([(pd[:, 0:H], T.sw[:], below)], ["sw"] + bk, k("pd"))
            tt(b["pt"][:, 0:H], below, b["su"][:, 0:H], OP.max, bk + k("su"), k("pta"))
            tt(b["pt"][:, H:M], b["su"][:, H:M], pd[:, 0:H], OP.max, k("su"), k("pd", "ptb"))
            table, tk = b["pt"], k("pta", "ptb")
        act(T.ga[:], table[:].indirect(ls[:, 32:K]), tk + ["ls" + n], ["ga"])
        for j in range(2):
            lo, hi = 512 * j, 512 * j + 512
            key = "yo%s_%d" % (n, j)
            if j == 0:
                tt(yo[:, lo:hi], table[:].indirect(ls[:, 0:32]), b["yl"][:, lo:hi], OP.max,
                   tk + ["ls" + n] + k("yl"), [key])
            else:
                tt(yo[:, lo:hi], T.ga[:], pc[:], OP.max, ["ga"] + k("ylp"), ["pc" + s, key])
            if L == 1:
                for h in range(2):
                    dma("SA"[h], T.y[64 * st:64 * st + 64, S * h + lo:S * h + hi], yo[64 * h:64 * h + 64, lo:hi],
                        [key], ["out%d%d%d" % (st, h, j)], "st%d%d%d" % (st, h, j))
        if L == 0:
            mm(wrap(pa, b["zw"], yo), ["yo%s_0" % n, "yo%s_1" % n] + k("zw"), k("pa"))

    for L in range(2):
        for st in range(2):
            layer(st, L)
    rec("S", None, ["out%d%d%d" % (st, h, j) for st in range(2) for h in range(2) for j in range(2)], [],
        kind="end", tag="end")
    return ops, sent[0]


def rank_program(g, core, T, topo):
    rank = T.rank_of(core)
    if rank is None:
        return
    ops, sent = build(g, core, T, topo, rank)
    place = {t: n for n, t in enumerate(ORDER.split())}
    ops.sort(key=lambda o: place[o["tag"]])
    emit(g, T, ops)
    g.wait_ge(T.sem.sent, sent)
